import numpy as np
import ml_dtypes


def mxq(x, axis, fmt="e4m3"):
    dtype, down = {"e4m3": (ml_dtypes.float8_e4m3fn, 7), "e5m2": (ml_dtypes.float8_e5m2, 14)}[fmt]
    v = np.moveaxis(np.asarray(x, np.float32).astype(ml_dtypes.bfloat16).astype(np.float64), axis, -1)
    blocks = v.reshape(v.shape[:-1] + (-1, 32))
    amax = np.abs(blocks).max(-1, keepdims=True)
    byte = np.maximum(np.where(amax > 0, np.frexp(amax)[1] - 1 + 127, 0) - down, 1)
    scale = np.exp2(byte - 127.0)
    codes = (blocks / scale).astype(np.float32).astype(dtype).astype(np.float64)
    return np.moveaxis((codes * scale).reshape(v.shape), -1, axis)


WIDE = False


def mx_kscale(k):
    if not WIDE:
        return np.ones(k)
    levels = np.array([10, -10, 5, -5, 0])
    if k % 512:
        return np.exp2(np.random.permutation(np.resize(levels, k // 32))).repeat(32)
    a = np.empty((k // 512, 16))
    for p in range(k // 512):
        a[p, :8] = np.random.permutation(np.resize(levels, 8))
        for g in range(8):
            far = levels[np.abs(levels - a[p, g]) >= 10]
            a[p, g + 8] = far[np.random.randint(len(far))]
    return np.exp2(a.ravel()).repeat(32)


def f64(x):
    return np.asarray(x).astype(np.float64)


def striped(idx):
    return np.tile(idx.reshape(-1, 16).T, (8, 1)).astype(np.uint16)


def unstriped(offs):
    return offs[:16].T.reshape(-1).astype(np.int64)


def striped8(idx):
    return np.concatenate([x.reshape(-1, 16).T for x in idx]).astype(np.uint16)


def runs(offs, k):
    lists = np.stack([offs[16 * r : 16 * r + 16].T.reshape(-1) for r in range(8)]).astype(np.int64)
    return lists[np.arange(k) % 512 // 64]


def pack_weight(w):
    k, n = w.shape
    w = f64(np.asarray(w, np.float32).astype(ml_dtypes.bfloat16)).reshape(k // 32, 32, n)
    amax = np.abs(w).max(1)
    byte = np.clip(np.where(amax > 0, np.frexp(amax)[1] - 1 + 127 - 7, 1), 1, 254)
    scaled = (w * np.exp2(127.0 - byte)[:, None, :]).reshape(k, n).astype(np.float32)
    words = np.ascontiguousarray(scaled.reshape(k // 512, 128, 4, n).transpose(0, 1, 3, 2)).astype(ml_dtypes.float8_e4m3fn).view(np.uint8)
    return words, np.ascontiguousarray(byte.astype(np.uint8).reshape(k // 512, 16, n))


def unpack_weight(words, scales):
    g, p, n, _ = words.shape
    vals = np.ascontiguousarray(words).view(ml_dtypes.float8_e4m3fn).astype(np.float64) * np.repeat(np.exp2(scales.astype(np.float64) - 127.0), 8, axis=1)[..., None]
    return vals.transpose(0, 1, 3, 2).reshape(g * 512, n)


def sigmoid(v):
    return 1.0 / (1.0 + np.exp(-np.maximum(v, -700.0)))


K, T, S, V, H, W = 512, 2048, 512, 512, 512, 256


def setup_inputs():
    n = np.random.standard_normal
    s = mx_kscale(K)[:, None]
    u = mx_kscale(S)
    packed_xT = pack_weight(n((K, T)) * s)
    perm = np.stack([np.random.permutation(V) for _ in range(8)])
    return {
        "x_words": packed_xT[0],
        "x_scales": packed_xT[1],
        "w1": (n((K, H)) / np.sqrt(K) / s).astype(np.float32),
        "w2": (n((K, H)) / np.sqrt(K) / s).astype(np.float32),
        "w3": (n((K, H)) / np.sqrt(K) / s).astype(np.float32),
        "ga": (np.random.uniform(0.5, 1.5, (H, 1)) * u[:, None]).astype(np.float32),
        "gb": (np.random.uniform(0.5, 1.5, (H, 1)) / u[:, None]).astype(np.float32),
        "offs": striped(np.random.permutation(T)[:S]),
        "two": striped(np.random.permutation(T)[:S]),
        "n1": striped8(np.stack([np.random.permutation(S) for _ in range(8)])),
        "n2": striped8(np.stack([np.random.permutation(S) for _ in range(8)])),
        "three": striped(np.random.permutation(T)[:V]),
        "n3": striped8(perm[:, :W]),
        "n4": striped8(perm[:, W:]),
        "n5": striped8(np.stack([np.random.permutation(V) for _ in range(8)])),
    }


def reference(x_words, x_scales, w1, w2, w3, ga, gb, offs, two, n1, n2, three, n3, n4, n5):
    xq = unpack_weight(x_words, x_scales)[:, unstriped(offs)]
    y = mxq(f64(w1), 0, "e4m3").T @ xq
    x_two = unpack_weight(x_words, x_scales)[:, unstriped(two)]
    d = mxq(f64(w2), 0, "e4m3").T @ x_two
    z = f64(ga) * (np.maximum(y, d[np.arange(H)[:, None], runs(n2, H)]) - (np.minimum(y[np.arange(H)[:, None], runs(n1, H)], d)))
    x_three = unpack_weight(x_words, x_scales)[:, unstriped(three)]
    b = mxq(f64(w3), 0, "e4m3").T @ x_three
    pa = b[np.arange(H)[:, None], runs(n3, H)]
    pb = b[np.arange(H)[:, None], runs(n4, H)]
    ra = pa * sigmoid(pb)
    ds = b.copy()
    ds[np.arange(H)[:, None], runs(n4, H)] = ra
    z2 = f64(gb) * ds
    s = 0.0625 * ((mxq(z, 0, "e4m3").T @ mxq(z2, 0, "e4m3")))
    return np.maximum(s, s[np.arange(S)[:, None], runs(n5, S)])

@@ -1,0 +1,227 @@
+from contextlib import ExitStack
+
+import concourse.mybir as mybir
+from concourse.masks import make_identity
+
+F32 = mybir.dt.float32
+BF16 = mybir.dt.bfloat16
+I32 = mybir.dt.int32
+U32 = mybir.dt.uint32
+U16 = mybir.dt.uint16
+U8 = mybir.dt.uint8
+FP8X4 = mybir.dt.float8_e4m3fn_x4
+ALU = mybir.AluOpType
+ACT = mybir.ActivationFunctionType
+
+P = 128
+PACK = 4
+T = 2048
+N = 512
+HALF = N // 2
+WIDE = 2 * N
+SPLIT = 320
+
+FLOPS = 4 * 2 * 512 * 512 * 512
+
+
+def tile_picked_twkmaxbfoldbig_none_p_kernel(
+    tc, x_words, x_scales, w1, w2, w3, ga, gb, offs, two, n1, n2, three, n3, n4, n5, out
+):
+    nc = tc.nc
+    with ExitStack() as ctx:
+        keep = ctx.enter_context(tc.tile_pool(name="keep", bufs=1))
+        psum = ctx.enter_context(tc.psum_pool(name="psum", bufs=1))
+
+        def sbuf(name, shape, dtype):
+            return keep.tile(shape, dtype, name=name, align_bytes=64)
+
+        def bank(name, shape):
+            return psum.tile(shape, F32, name=name, tag="ring", bufs=4)
+
+        def load_list(name, src):
+            tile = sbuf(name, list(src.shape), U16)
+            nc.sync.dma_start(tile[:], src)
+            return tile
+
+        def load_weight(name, w, half):
+            raw = sbuf(f"{name}_raw{half}", [P, PACK, HALF], F32)
+            cols = slice(half * HALF, (half + 1) * HALF)
+            nc.sync.dma_start(raw[:], w.rearrange("(p j) c -> p j c", j=PACK)[:, :, cols])
+            return raw
+
+        scale_rows = sbuf("scale_rows", [P, T], U8)
+        nc.gpsimd.memset(scale_rows[:].bitcast(I32), 0)
+        warm = sbuf("warm", [P, 2], F32)
+        nc.gpsimd.memset(warm[:, 0:1], 0.0)
+        nc.scalar.activation(warm[:, 1:2], warm[:, 0:1], ACT.Sigmoid)
+
+        three_t = load_list("three_t", three)
+        w3_raw = [load_weight("w3", w3, 0)]
+        for q in range(4):
+            nc.sync.dma_start(scale_rows[32 * q : 32 * q + 4, :].bitcast(I32), x_scales[0, 4 * q : 4 * q + 4, :].bitcast(I32))
+        offs_t = load_list("offs_t", offs)
+        two_t = load_list("two_t", two)
+        words = sbuf("words", [P, T], U32)
+        w3_raw.append(load_weight("w3", w3, 1))
+        nc.sync.dma_start(words[:].bitcast(I32), x_words[0].rearrange("p c r -> p (c r)").bitcast(I32))
+        n4_t = load_list("n4_t", n4)
+        n3_t = load_list("n3_t", n3)
+        w1_raw = [load_weight("w1", w1, h) for h in range(2)]
+        w2_raw = [load_weight("w2", w2, h) for h in range(2)]
+        n2_t = load_list("n2_t", n2)
+        n1_t = load_list("n1_t", n1)
+        n5_t = load_list("n5_t", n5)
+
+        ga_t = sbuf("ga_t", [P, PACK], F32)
+        gb_t = sbuf("gb_t", [P, PACK], F32)
+        nc.gpsimd.dma_start(ga_t[:], ga.rearrange("(p t) o -> p (t o)", t=PACK))
+        nc.gpsimd.dma_start(gb_t[:], gb.rearrange("(p t) o -> p (t o)", t=PACK))
+        sign2 = sbuf("sign2", [P, PACK], F32)
+        sign = sbuf("sign", [P, PACK], F32)
+        ga_abs = sbuf("ga_abs", [P, PACK], F32)
+        ga_neg = sbuf("ga_neg", [P, PACK], F32)
+        gb_signed = sbuf("gb_signed", [P, PACK], F32)
+        nc.gpsimd.tensor_scalar(sign2[:], ga_t[:], 0.0, 2.0, ALU.is_ge, ALU.mult)
+        nc.gpsimd.tensor_scalar(sign[:], sign2[:], 1.0, -1.0, ALU.mult, ALU.add)
+        nc.gpsimd.tensor_tensor(ga_abs[:], ga_t[:], sign[:], ALU.mult)
+        nc.gpsimd.tensor_scalar(ga_neg[:], ga_abs[:], -1.0, 0.0, ALU.mult, ALU.add)
+        nc.gpsimd.tensor_tensor(gb_signed[:], gb_t[:], sign[:], ALU.mult)
+        ident = sbuf("ident", [P, P], F32)
+        make_identity(nc, ident[:])
+
+        y_win = [sbuf(f"y_win{t}", [P, WIDE], F32) for t in range(PACK)]
+        d_win = [sbuf(f"d_win{t}", [P, WIDE], F32) for t in range(PACK)]
+
+        def pick_bytes(name, lst):
+            tile = sbuf(name, [P, N], U8)
+            nc.vector.tensor_copy(tile[:], scale_rows[:].indirect(lst[:]))
+            return tile
+
+        def pick_words(name, lst):
+            tile = sbuf(name, [P, N], U32)
+            nc.vector.tensor_copy(tile[:], words[:].indirect(lst[:]))
+            return tile
+
+        def quantize(name, grouped):
+            codes = sbuf(f"{name}_codes", [P, N], U32)
+            scales = sbuf(f"{name}_scales", [P, N], U8)
+            nc.vector.quantize_mx(out=codes[:].bitcast(FP8X4), scales=scales[:], in_=grouped[:])
+            return codes, scales
+
+        def group_weight(name, raw):
+            grouped = sbuf(f"{name}_grouped", [P, PACK * N], BF16)
+            view = grouped[:].rearrange("p (t m j) -> p m j t", t=PACK, j=PACK)
+            for h in range(2):
+                nc.scalar.copy(view[:, h * 64 : (h + 1) * 64], raw[h][:].rearrange("p j (m t) -> p m j t", t=PACK))
+            return grouped
+
+        def product(name, stat, mov, t):
+            acc = bank(name, [P, N])
+            cols = slice(t * P, (t + 1) * P)
+            nc.tensor.matmul_mx(
+                out=acc[:], lhsT=stat[0][:, cols].bitcast(FP8X4), lhsT_scale=stat[1][:, cols],
+                rhs=mov[0][:].bitcast(FP8X4), rhs_scale=mov[1][:], start=True, stop=True,
+            )
+            return acc
+
+        xb_bytes = pick_bytes("xb_bytes", three_t)
+        xy_bytes = pick_bytes("xy_bytes", offs_t)
+        xd_bytes = pick_bytes("xd_bytes", two_t)
+        w3q = quantize("w3", group_weight("w3", w3_raw))
+        xb = (pick_words("xb_words", three_t), xb_bytes)
+        xy = (pick_words("xy_words", offs_t), xy_bytes)
+        xd = (pick_words("xd_words", two_t), xd_bytes)
+
+        dg = sbuf("dg", [P, N], F32)
+        yg = sbuf("yg", [P, N], F32)
+        z2_planes = sbuf("z2_planes", [P, PACK, N], BF16)
+        b_win = [sbuf(f"b_win{t}", [P, N], F32) for t in range(PACK)]
+        gate = [sbuf(f"gate{t}", [P, HALF], F32) for t in range(PACK)]
+
+        def make_b(t):
+            acc = product(f"b{t}", w3q, xb, t)
+            nc.scalar.copy(b_win[t][:], acc[:])
+            nc.scalar.activation(gate[t][:], b_win[t][:].indirect(n4_t[:]), ACT.Sigmoid)
+
+        def pair_up(t, pa):
+            nc.vector.tensor_copy(pa, b_win[t][:].indirect(n3_t[:]))
+            nc.vector.tensor_tensor(b_win[t][:].indirect(n4_t[:]), pa, gate[t][:], ALU.mult)
+
+        def scale_b(t):
+            nc.scalar.activation(z2_planes[:, t, :], b_win[t][:], ACT.Copy, scale=gb_signed[:, t : t + 1])
+
+        pa_tiles = [sbuf(f"pa{t}", [P, HALF], F32) for t in range(PACK - 1)]
+        for t in range(PACK - 1):
+            make_b(t)
+            pair_up(t, pa_tiles[t][:])
+
+        w1q = quantize("w1", group_weight("w1", w1_raw))
+        w2q = quantize("w2", group_weight("w2", w2_raw))
+
+        zT = [[psum.tile([P, 2, 2, P], F32, name=f"zT{u}{h}", tag=f"zT{u}{h}") for h in range(2)] for u in range(2)]
+        back = [None, None]
+
+        def turn_back(u):
+            for h in range(2):
+                rows = sbuf(f"zT_bf{u}{h}", [P, N], BF16)
+                nc.scalar.copy(
+                    rows[:].rearrange("k (c p e) -> k c p e", c=2, e=2),
+                    zT[u][h][:].rearrange("k c e p -> k c p e"),
+                )
+                row_words = rows[:].bitcast(F32)
+                if u == 0:
+                    back[h] = psum.tile([P, 2, HALF], F32, name=f"back{h}", tag=f"zT0{h}")
+                for cc in range(2):
+                    nc.tensor.transpose(back[h][:, u, cc * P : (cc + 1) * P], row_words[:, cc * P : (cc + 1) * P], ident[:])
+
+        for t in range(PACK):
+            acc_d = product(f"d{t}", w2q, xd, t)
+            nc.scalar.activation(d_win[t][:, :N], acc_d[:], ACT.Copy, scale=ga_neg[:, t : t + 1])
+            acc_y = product(f"y{t}", w1q, xy, t)
+            nc.scalar.activation(y_win[t][:, :N], acc_y[:], ACT.Copy, scale=ga_abs[:, t : t + 1])
+            nc.vector.tensor_copy(dg[:], d_win[t][:].indirect(n2_t[:]))
+            nc.vector.tensor_copy(yg[:], y_win[t][:].indirect(n1_t[:]))
+            hi = sbuf(f"hi{t}", [P, N], F32)
+            lo = sbuf(f"lo{t}", [P, N], F32)
+            nc.vector.scalar_tensor_tensor(hi[:], dg[:], -1.0, y_win[t][:, :N], ALU.mult, ALU.max)
+            nc.vector.scalar_tensor_tensor(lo[:], yg[:], -1.0, d_win[t][:, :N], ALU.mult, ALU.max)
+            for c in range(PACK):
+                cols = slice(c * P, (c + 1) * P)
+                dst = zT[t // 2][c // 2][:, c % 2, t % 2, :]
+                nc.tensor.matmul(dst, hi[:, cols], ident[:], is_transpose=True, start=True, stop=False)
+                nc.tensor.matmul(dst, lo[:, cols], ident[:], is_transpose=True, start=False, stop=True)
+            if t == 1:
+                make_b(PACK - 1)
+                for tb in range(PACK - 1):
+                    scale_b(tb)
+                turn_back(0)
+
+        pair_up(PACK - 1, dg[:, :HALF])
+        turn_back(1)
+
+        z_grouped = sbuf("z_grouped", [P, PACK * N], BF16)
+        z_words = z_grouped[:].bitcast(F32).rearrange("p (t m u) -> p t m u", t=PACK, u=2)
+        for h in range(2):
+            nc.scalar.copy(z_words[:, :, h * 64 : (h + 1) * 64, :], back[h][:].rearrange("p u (m t) -> p t m u", t=PACK))
+        zq = quantize("z", z_grouped)
+
+        scale_b(PACK - 1)
+        z2_grouped = sbuf("z2_grouped", [P, PACK * N], BF16)
+        dst = z2_grouped[:].rearrange("p (c i t) -> p c t i", i=4, t=PACK)
+        src = z2_planes[:].rearrange("p t (c i) -> p c t i", i=4)
+        nc.vector.tensor_copy(dst[:, : SPLIT // 4], src[:, : SPLIT // 4])
+        nc.scalar.copy(dst[:, SPLIT // 4 :], src[:, SPLIT // 4 :])
+        z2q = quantize("z2", z2_grouped)
+
+        out_rows = out.rearrange("(p t) v -> t p v", t=PACK)
+        for t in range(PACK):
+            acc = product(f"s{t}", zq, z2q, t)
+            nc.scalar.activation(y_win[t][:, :N], acc[:], ACT.Copy, scale=0.0625)
+        sg = [dg, yg]
+        for t in range(PACK + 1):
+            if t < PACK:
+                nc.vector.tensor_copy(sg[t % 2][:], y_win[t][:].indirect(n5_t[:]))
+            if t > 0:
+                res = d_win[t - 1][:, :N]
+                nc.vector.tensor_tensor(res, sg[(t - 1) % 2][:], y_win[t - 1][:, :N], ALU.max)
+                nc.sync.dma_start(out_rows[t - 1], res)

@@ -19,7 +19,6 @@ T = 2048
 N = 512
 HALF = N // 2
 WIDE = 2 * N
-SPLIT = 320
 
 FLOPS = 4 * 2 * 512 * 512 * 512
 
@@ -36,7 +35,7 @@ def tile_picked_twkmaxbfoldbig_none_p_kernel(
             return keep.tile(shape, dtype, name=name, align_bytes=64)
 
         def bank(name, shape):
-            return psum.tile(shape, F32, name=name, tag="ring", bufs=4)
+            return psum.tile(shape, F32, name=name, tag="ring", bufs=2)
 
         def load_list(name, src):
             tile = sbuf(name, list(src.shape), U16)
@@ -50,19 +49,19 @@ def tile_picked_twkmaxbfoldbig_none_p_kernel(
             return raw
 
         scale_rows = sbuf("scale_rows", [P, T], U8)
-        nc.gpsimd.memset(scale_rows[:].bitcast(I32), 0)
+        nc.vector.memset(scale_rows[:, : T // 2].bitcast(I32), 0)
+        nc.gpsimd.memset(scale_rows[:, T // 2 :].bitcast(I32), 0)
         warm = sbuf("warm", [P, 2], F32)
         nc.gpsimd.memset(warm[:, 0:1], 0.0)
         nc.scalar.activation(warm[:, 1:2], warm[:, 0:1], ACT.Sigmoid)
 
         three_t = load_list("three_t", three)
-        w3_raw = [load_weight("w3", w3, 0)]
-        for q in range(4):
-            nc.sync.dma_start(scale_rows[32 * q : 32 * q + 4, :].bitcast(I32), x_scales[0, 4 * q : 4 * q + 4, :].bitcast(I32))
         offs_t = load_list("offs_t", offs)
         two_t = load_list("two_t", two)
+        for q in range(4):
+            nc.sync.dma_start(scale_rows[32 * q : 32 * q + 4, :].bitcast(I32), x_scales[0, 4 * q : 4 * q + 4, :].bitcast(I32))
         words = sbuf("words", [P, T], U32)
-        w3_raw.append(load_weight("w3", w3, 1))
+        w3_raw = [load_weight("w3", w3, h) for h in range(2)]
         nc.sync.dma_start(words[:].bitcast(I32), x_words[0].rearrange("p c r -> p (c r)").bitcast(I32))
         n4_t = load_list("n4_t", n4)
         n3_t = load_list("n3_t", n3)
@@ -132,8 +131,8 @@ def tile_picked_twkmaxbfoldbig_none_p_kernel(
         xy = (pick_words("xy_words", offs_t), xy_bytes)
         xd = (pick_words("xd_words", two_t), xd_bytes)
 
-        dg = sbuf("dg", [P, N], F32)
-        yg = sbuf("yg", [P, N], F32)
+        dgs = [sbuf(f"dg{i}", [P, N], F32) for i in range(2)]
+        ygs = [sbuf(f"yg{i}", [P, N], F32) for i in range(2)]
         z2_planes = sbuf("z2_planes", [P, PACK, N], BF16)
         b_win = [sbuf(f"b_win{t}", [P, N], F32) for t in range(PACK)]
         gate = [sbuf(f"gate{t}", [P, HALF], F32) for t in range(PACK)]
@@ -143,85 +142,139 @@ def tile_picked_twkmaxbfoldbig_none_p_kernel(
             nc.scalar.copy(b_win[t][:], acc[:])
             nc.scalar.activation(gate[t][:], b_win[t][:].indirect(n4_t[:]), ACT.Sigmoid)
 
-        def pair_up(t, pa):
+        def fetch_pa(t, pa):
             nc.vector.tensor_copy(pa, b_win[t][:].indirect(n3_t[:]))
+
+        def put_back(t, pa):
             nc.vector.tensor_tensor(b_win[t][:].indirect(n4_t[:]), pa, gate[t][:], ALU.mult)
+
+        def pair_up(t, pa):
+            fetch_pa(t, pa)
+            put_back(t, pa)
 
         def scale_b(t):
             nc.scalar.activation(z2_planes[:, t, :], b_win[t][:], ACT.Copy, scale=gb_signed[:, t : t + 1])
 
-        pa_tiles = [sbuf(f"pa{t}", [P, HALF], F32) for t in range(PACK - 1)]
-        for t in range(PACK - 1):
+        pa_tiles = [sbuf(f"pa{t}", [P, HALF], F32) for t in range(2)]
+        for t in range(2):
             make_b(t)
             pair_up(t, pa_tiles[t][:])
 
-        w1q = quantize("w1", group_weight("w1", w1_raw))
-        w2q = quantize("w2", group_weight("w2", w2_raw))
+        w1_grouped = group_weight("w1", w1_raw)
+        w1q = quantize("w1", w1_grouped)
+        w2_grouped = group_weight("w2", w2_raw)
+        w2q = quantize("w2", w2_grouped)
+        make_b(2)
+        pair_up(2, w2_grouped[:].bitcast(F32)[:, :HALF])
 
-        zT = [[psum.tile([P, 2, 2, P], F32, name=f"zT{u}{h}", tag=f"zT{u}{h}") for h in range(2)] for u in range(2)]
-        back = [None, None]
+        zT = [psum.tile([P, PACK, P], F32, name=f"zT{c}", tag=f"zT{c}") for c in range(PACK)]
+        back = [psum.tile([P, 2, HALF], F32, name=f"back{h}") for h in range(2)]
+        hi = [sbuf(f"hi{t}", [P, N], F32) for t in range(PACK)]
+        lo = [sbuf(f"lo{t}", [P, N], F32) for t in range(PACK)]
 
-        def turn_back(u):
-            for h in range(2):
-                rows = sbuf(f"zT_bf{u}{h}", [P, N], BF16)
-                nc.scalar.copy(
-                    rows[:].rearrange("k (c p e) -> k c p e", c=2, e=2),
-                    zT[u][h][:].rearrange("k c e p -> k c p e"),
-                )
-                row_words = rows[:].bitcast(F32)
-                if u == 0:
-                    back[h] = psum.tile([P, 2, HALF], F32, name=f"back{h}", tag=f"zT0{h}")
-                for cc in range(2):
-                    nc.tensor.transpose(back[h][:, u, cc * P : (cc + 1) * P], row_words[:, cc * P : (cc + 1) * P], ident[:])
-
-        for t in range(PACK):
+        def make_yd(t):
             acc_d = product(f"d{t}", w2q, xd, t)
             nc.scalar.activation(d_win[t][:, :N], acc_d[:], ACT.Copy, scale=ga_neg[:, t : t + 1])
             acc_y = product(f"y{t}", w1q, xy, t)
             nc.scalar.activation(y_win[t][:, :N], acc_y[:], ACT.Copy, scale=ga_abs[:, t : t + 1])
-            nc.vector.tensor_copy(dg[:], d_win[t][:].indirect(n2_t[:]))
-            nc.vector.tensor_copy(yg[:], y_win[t][:].indirect(n1_t[:]))
-            hi = sbuf(f"hi{t}", [P, N], F32)
-            lo = sbuf(f"lo{t}", [P, N], F32)
-            nc.vector.scalar_tensor_tensor(hi[:], dg[:], -1.0, y_win[t][:, :N], ALU.mult, ALU.max)
-            nc.vector.scalar_tensor_tensor(lo[:], yg[:], -1.0, d_win[t][:, :N], ALU.mult, ALU.max)
-            for c in range(PACK):
-                cols = slice(c * P, (c + 1) * P)
-                dst = zT[t // 2][c // 2][:, c % 2, t % 2, :]
-                nc.tensor.matmul(dst, hi[:, cols], ident[:], is_transpose=True, start=True, stop=False)
-                nc.tensor.matmul(dst, lo[:, cols], ident[:], is_transpose=True, start=False, stop=True)
-            if t == 1:
-                make_b(PACK - 1)
-                for tb in range(PACK - 1):
-                    scale_b(tb)
-                turn_back(0)
 
-        pair_up(PACK - 1, dg[:, :HALF])
+        def look_up(t):
+            dg, yg = dgs[t % 2], ygs[t % 2]
+            nc.vector.tensor_tensor(yg[:], y_win[t][:].indirect(n1_t[:]), d_win[t][:, :N], ALU.add)
+            nc.vector.tensor_tensor(dg[:], d_win[t][:].indirect(n2_t[:]), y_win[t][:, :N], ALU.add)
+
+        def clip(t):
+            dg, yg = dgs[t % 2], ygs[t % 2]
+            nc.vector.tensor_scalar(lo[t][:], yg[:], -1.0, 0.0, ALU.mult, ALU.max)
+            nc.scalar.activation(hi[t][:], dg[:], ACT.Relu, scale=-1.0)
+
+        def add_up(t):
+            terms = [y_win[t], d_win[t], lo[t], hi[t]]
+            for i, term in enumerate(terms):
+                for c in range(PACK):
+                    cols = slice(c * P, (c + 1) * P)
+                    nc.tensor.matmul(zT[c][:, t, :], term[:, cols], ident[:], is_transpose=True, start=(i == 0), stop=(i == 3))
+
+        def turn_back(u):
+            for c in range(PACK):
+                rows = sbuf(f"zT_bf{u}{c}", [P, HALF], BF16)
+                nc.scalar.copy(
+                    rows[:].rearrange("k (p e) -> k p e", e=2),
+                    zT[c][:, 2 * u : 2 * u + 2, :].rearrange("k e p -> k p e"),
+                )
+                nc.tensor.transpose(back[c // 2][:, u, (c % 2) * P : (c % 2 + 1) * P], rows[:].bitcast(F32), ident[:])
+
+        make_yd(0)
+        make_yd(1)
+        look_up(0)
+        clip(0)
+        make_yd(2)
+        add_up(0)
+        look_up(1)
+        clip(1)
+        make_yd(3)
+        add_up(1)
+        make_b(3)
+        turn_back(0)
+        look_up(2)
+        clip(2)
+        add_up(2)
+        for t in range(PACK - 1):
+            scale_b(t)
+        look_up(3)
+        pa_last = d_win[3][:, N : N + HALF]
+        fetch_pa(3, pa_last)
+        clip(3)
+        add_up(3)
+        put_back(3, pa_last)
         turn_back(1)
 
         z_grouped = sbuf("z_grouped", [P, PACK * N], BF16)
         z_words = z_grouped[:].bitcast(F32).rearrange("p (t m u) -> p t m u", t=PACK, u=2)
         for h in range(2):
             nc.scalar.copy(z_words[:, :, h * 64 : (h + 1) * 64, :], back[h][:].rearrange("p u (m t) -> p t m u", t=PACK))
-        zq = quantize("z", z_grouped)
 
-        scale_b(PACK - 1)
+        halves = [slice(0, HALF), slice(HALF, N)]
+        for cols in halves:
+            nc.vector.tensor_scalar(z2_planes[:, 3, cols], b_win[3][:, cols], gb_signed[:, 3:4], None, ALU.mult)
         z2_grouped = sbuf("z2_grouped", [P, PACK * N], BF16)
-        dst = z2_grouped[:].rearrange("p (c i t) -> p c t i", i=4, t=PACK)
-        src = z2_planes[:].rearrange("p t (c i) -> p c t i", i=4)
-        nc.vector.tensor_copy(dst[:, : SPLIT // 4], src[:, : SPLIT // 4])
-        nc.scalar.copy(dst[:, SPLIT // 4 :], src[:, SPLIT // 4 :])
-        z2q = quantize("z2", z2_grouped)
+        dst = z2_grouped[:].rearrange("p (h c i t) -> p h c t i", h=2, i=4, t=PACK)
+        src = z2_planes[:].rearrange("p t (h c i) -> p h c t i", h=2, i=4)
+        for h in range(2):
+            nc.vector.tensor_copy(dst[:, h], src[:, h])
+
+        def quantize_pieces(name, grouped, edges):
+            codes = sbuf(f"{name}_codes", [P, N], U32)
+            scales = sbuf(f"{name}_scales", [P, N], U8)
+            for c0, c1 in zip(edges, edges[1:]):
+                nc.vector.quantize_mx(
+                    out=codes[:, c0:c1].bitcast(FP8X4), scales=scales[:, c0:c1], in_=grouped[:, PACK * c0 : PACK * c1]
+                )
+            return codes, scales
+
+        z2q = quantize_pieces("z2", z2_grouped, [0, HALF, N])
+        zq = quantize_pieces("z", z_grouped, [0, P, 2 * P, N])
 
         out_rows = out.rearrange("(p t) v -> t p v", t=PACK)
         for t in range(PACK):
-            acc = product(f"s{t}", zq, z2q, t)
-            nc.scalar.activation(y_win[t][:, :N], acc[:], ACT.Copy, scale=0.0625)
-        sg = [dg, yg]
+            rows = slice(t * P, (t + 1) * P)
+            for i, cols in enumerate(halves if t == 0 else [slice(0, N)]):
+                width = cols.stop - cols.start
+                if t == 0:
+                    acc = bank(f"s0{i}", [P, width])
+                else:
+                    acc = psum.tile([P, width], F32, name=f"s{t}", tag=f"zT{t}")
+                nc.tensor.matmul_mx(
+                    out=acc[:], lhsT=zq[0][:, rows].bitcast(FP8X4), lhsT_scale=zq[1][:, rows],
+                    rhs=z2q[0][:, cols].bitcast(FP8X4), rhs_scale=z2q[1][:, cols], start=True, stop=True,
+                )
+                nc.scalar.activation(y_win[t][:, cols], acc[:], ACT.Copy, scale=0.0625)
+        sg = dgs + ygs
         for t in range(PACK + 1):
             if t < PACK:
-                nc.vector.tensor_copy(sg[t % 2][:], y_win[t][:].indirect(n5_t[:]))
+                nc.vector.tensor_copy(sg[t][:], y_win[t][:].indirect(n5_t[:]))
             if t > 0:
-                res = d_win[t - 1][:, :N]
-                nc.vector.tensor_tensor(res, sg[(t - 1) % 2][:], y_win[t - 1][:, :N], ALU.max)
-                nc.sync.dma_start(out_rows[t - 1], res)
+                for cols in halves if t == PACK else [slice(0, N)]:
+                    res = d_win[t - 1][:, cols]
+                    nc.vector.tensor_tensor(res, sg[t - 1][:, cols], y_win[t - 1][:, cols], ALU.max)
+                    nc.sync.dma_start(out_rows[t - 1][:, cols], res)

@@ -35,18 +35,22 @@ def tile_picked_twkmaxbfoldbig_none_p_kernel(
             return keep.tile(shape, dtype, name=name, align_bytes=64)
 
         def bank(name, shape):
-            return psum.tile(shape, F32, name=name, tag="ring", bufs=2)
+            return psum.tile(shape, F32, name=name, tag="ring", bufs=4)
 
         def load_list(name, src):
             tile = sbuf(name, list(src.shape), U16)
             nc.sync.dma_start(tile[:], src)
             return tile
 
-        def load_weight(name, w, half):
-            raw = sbuf(f"{name}_raw{half}", [P, PACK, HALF], F32)
-            cols = slice(half * HALF, (half + 1) * HALF)
-            nc.sync.dma_start(raw[:], w.rearrange("(p j) c -> p j c", j=PACK)[:, :, cols])
-            return raw
+        def load_weight(name, w, pieces):
+            rows = w.rearrange("(p j) c -> p j c", j=PACK)
+            width = N // pieces
+            halves = []
+            for i in range(pieces):
+                raw = sbuf(f"{name}_raw{i}", [P, PACK, width], F32)
+                nc.sync.dma_start(raw[:], rows[:, :, i * width : (i + 1) * width])
+                halves.extend(raw[:, :, c : c + HALF] for c in range(0, width, HALF))
+            return halves
 
         scale_rows = sbuf("scale_rows", [P, T], U8)
         nc.vector.memset(scale_rows[:, : T // 2].bitcast(I32), 0)
@@ -61,12 +65,12 @@ def tile_picked_twkmaxbfoldbig_none_p_kernel(
         for q in range(4):
             nc.sync.dma_start(scale_rows[32 * q : 32 * q + 4, :].bitcast(I32), x_scales[0, 4 * q : 4 * q + 4, :].bitcast(I32))
         words = sbuf("words", [P, T], U32)
-        w3_raw = [load_weight("w3", w3, h) for h in range(2)]
+        w3_raw = load_weight("w3", w3, 2)
         nc.sync.dma_start(words[:].bitcast(I32), x_words[0].rearrange("p c r -> p (c r)").bitcast(I32))
         n4_t = load_list("n4_t", n4)
         n3_t = load_list("n3_t", n3)
-        w1_raw = [load_weight("w1", w1, h) for h in range(2)]
-        w2_raw = [load_weight("w2", w2, h) for h in range(2)]
+        w1_raw = load_weight("w1", w1, 2)
+        w2_raw = load_weight("w2", w2, 2)
         n2_t = load_list("n2_t", n2)
         n1_t = load_list("n1_t", n1)
         n5_t = load_list("n5_t", n5)
@@ -111,7 +115,7 @@ def tile_picked_twkmaxbfoldbig_none_p_kernel(
             grouped = sbuf(f"{name}_grouped", [P, PACK * N], BF16)
             view = grouped[:].rearrange("p (t m j) -> p m j t", t=PACK, j=PACK)
             for h in range(2):
-                nc.scalar.copy(view[:, h * 64 : (h + 1) * 64], raw[h][:].rearrange("p j (m t) -> p m j t", t=PACK))
+                nc.scalar.copy(view[:, h * 64 : (h + 1) * 64], raw[h].rearrange("p j (m t) -> p m j t", t=PACK))
             return grouped
 
         def product(name, stat, mov, t):
@@ -131,46 +135,48 @@ def tile_picked_twkmaxbfoldbig_none_p_kernel(
         xy = (pick_words("xy_words", offs_t), xy_bytes)
         xd = (pick_words("xd_words", two_t), xd_bytes)
 
-        dgs = [sbuf(f"dg{i}", [P, N], F32) for i in range(2)]
-        ygs = [sbuf(f"yg{i}", [P, N], F32) for i in range(2)]
-        z2_planes = sbuf("z2_planes", [P, PACK, N], BF16)
+        gap_tiles = [sbuf(f"gaps{i}", [P, WIDE], F32) for i in range(2)]
+        z2_planes = w2_raw[1].bitcast(BF16)
         b_win = [sbuf(f"b_win{t}", [P, N], F32) for t in range(PACK)]
-        gate = [sbuf(f"gate{t}", [P, HALF], F32) for t in range(PACK)]
+        gate = [w2_raw[1][:, 3, :] if t == 2 else sbuf(f"gate{t}", [P, HALF], F32)[:] for t in range(PACK)]
 
         def make_b(t):
             acc = product(f"b{t}", w3q, xb, t)
             nc.scalar.copy(b_win[t][:], acc[:])
-            nc.scalar.activation(gate[t][:], b_win[t][:].indirect(n4_t[:]), ACT.Sigmoid)
+
+        def make_gate(t):
+            nc.scalar.activation(gate[t], b_win[t][:].indirect(n4_t[:]), ACT.Sigmoid)
 
         def fetch_pa(t, pa):
             nc.vector.tensor_copy(pa, b_win[t][:].indirect(n3_t[:]))
 
         def put_back(t, pa):
-            nc.vector.tensor_tensor(b_win[t][:].indirect(n4_t[:]), pa, gate[t][:], ALU.mult)
-
-        def pair_up(t, pa):
-            fetch_pa(t, pa)
-            put_back(t, pa)
+            nc.vector.tensor_tensor(b_win[t][:].indirect(n4_t[:]), pa, gate[t], ALU.mult)
 
         def scale_b(t):
             nc.scalar.activation(z2_planes[:, t, :], b_win[t][:], ACT.Copy, scale=gb_signed[:, t : t + 1])
 
         pa_tiles = [sbuf(f"pa{t}", [P, HALF], F32) for t in range(2)]
-        for t in range(2):
-            make_b(t)
-            pair_up(t, pa_tiles[t][:])
+        for step in (make_b, make_gate):
+            for t in range(2):
+                step(t)
+        for step in (fetch_pa, put_back):
+            for t in range(2):
+                step(t, pa_tiles[t][:])
 
         w1_grouped = group_weight("w1", w1_raw)
-        w1q = quantize("w1", w1_grouped)
-        w2_grouped = group_weight("w2", w2_raw)
-        w2q = quantize("w2", w2_grouped)
         make_b(2)
-        pair_up(2, w2_grouped[:].bitcast(F32)[:, :HALF])
+        w1q = quantize("w1", w1_grouped)
+        pa_third = w1_grouped[:].bitcast(F32)[:, :HALF]
+        fetch_pa(2, pa_third)
+        w2q = quantize("w2", group_weight("w2", w2_raw))
+        make_gate(2)
+        put_back(2, pa_third)
 
-        zT = [psum.tile([P, PACK, P], F32, name=f"zT{c}", tag=f"zT{c}") for c in range(PACK)]
-        back = [psum.tile([P, 2, HALF], F32, name=f"back{h}") for h in range(2)]
-        hi = [sbuf(f"hi{t}", [P, N], F32) for t in range(PACK)]
-        lo = [sbuf(f"lo{t}", [P, N], F32) for t in range(PACK)]
+        zT = [[psum.tile([P, 2, 2, P], F32, name=f"zT{u}{h}", tag=f"zT{u}{h}") for h in range(2)] for u in range(2)]
+        back = [None, None]
+        halves = [slice(0, HALF), slice(HALF, N)]
+        clipped = [sbuf(f"clipped{t}", [P, WIDE], F32) for t in range(PACK)]
 
         def make_yd(t):
             acc_d = product(f"d{t}", w2q, xd, t)
@@ -179,100 +185,127 @@ def tile_picked_twkmaxbfoldbig_none_p_kernel(
             nc.scalar.activation(y_win[t][:, :N], acc_y[:], ACT.Copy, scale=ga_abs[:, t : t + 1])
 
         def look_up(t):
-            dg, yg = dgs[t % 2], ygs[t % 2]
-            nc.vector.tensor_tensor(yg[:], y_win[t][:].indirect(n1_t[:]), d_win[t][:, :N], ALU.add)
-            nc.vector.tensor_tensor(dg[:], d_win[t][:].indirect(n2_t[:]), y_win[t][:, :N], ALU.add)
+            gaps = gap_tiles[t % 2]
+            nc.vector.tensor_tensor(gaps[:, :N], y_win[t][:].indirect(n1_t[:]), d_win[t][:, :N], ALU.add)
+            nc.vector.tensor_tensor(gaps[:, N:], d_win[t][:].indirect(n2_t[:]), y_win[t][:, :N], ALU.add)
 
         def clip(t):
-            dg, yg = dgs[t % 2], ygs[t % 2]
-            nc.vector.tensor_scalar(lo[t][:], yg[:], -1.0, 0.0, ALU.mult, ALU.max)
-            nc.scalar.activation(hi[t][:], dg[:], ACT.Relu, scale=-1.0)
+            gaps = gap_tiles[t % 2]
+            if t < 2:
+                nc.scalar.activation(clipped[t][:], gaps[:], ACT.Relu, scale=-1.0)
+            else:
+                nc.vector.tensor_scalar(clipped[t][:, :N], gaps[:, :N], -1.0, 0.0, ALU.mult, ALU.max)
+                nc.scalar.activation(clipped[t][:, N:], gaps[:, N:], ACT.Relu, scale=-1.0)
 
-        def add_up(t):
-            terms = [y_win[t], d_win[t], lo[t], hi[t]]
-            for i, term in enumerate(terms):
-                for c in range(PACK):
-                    cols = slice(c * P, (c + 1) * P)
-                    nc.tensor.matmul(zT[c][:, t, :], term[:, cols], ident[:], is_transpose=True, start=(i == 0), stop=(i == 3))
-
-        def turn_back(u):
-            for c in range(PACK):
-                rows = sbuf(f"zT_bf{u}{c}", [P, HALF], BF16)
-                nc.scalar.copy(
-                    rows[:].rearrange("k (p e) -> k p e", e=2),
-                    zT[c][:, 2 * u : 2 * u + 2, :].rearrange("k e p -> k p e"),
+        def add_term(t, h, term, first=False, last=False):
+            for cc in range(2):
+                nc.tensor.matmul(
+                    zT[t // 2][h][:, cc, t % 2, :], term[:, cc * P : (cc + 1) * P], ident[:], is_transpose=True,
+                    start=(first and t % 2 == 0 and cc == 0), stop=(last and t % 2 == 1 and cc == 1),
                 )
-                nc.tensor.transpose(back[c // 2][:, u, (c % 2) * P : (c % 2 + 1) * P], rows[:].bitcast(F32), ident[:])
+
+        def add_plain(t):
+            for h, cols in enumerate(halves):
+                add_term(t, h, d_win[t][:, cols], first=True)
+                add_term(t, h, y_win[t][:, cols])
+
+        def add_clipped(t):
+            for h, cols in enumerate(halves):
+                add_term(t, h, clipped[t][:, :N][:, cols])
+            for h, cols in enumerate(halves):
+                add_term(t, h, clipped[t][:, N:][:, cols], last=True)
+
+        z2_grouped = sbuf("z2_grouped", [P, PACK * N], BF16)
+        z_grouped = sbuf("z_grouped", [P, PACK * N], BF16)
+        z_words = z_grouped[:].bitcast(F32).rearrange("p (t m u) -> p t m u", t=PACK, u=2)
+
+        def turn_back(u, h, rows):
+            nc.scalar.copy(
+                rows.rearrange("k (c p e) -> k c p e", c=2, e=2),
+                zT[u][h][:].rearrange("k c e p -> k c p e"),
+            )
+            if u == 0:
+                back[h] = psum.tile([P, 2, HALF], F32, name=f"back{h}", tag=f"zT0{h}")
+            row_words = rows.bitcast(F32)
+            for cc in range(2):
+                cols = slice(cc * P, (cc + 1) * P)
+                nc.tensor.transpose(back[h][:, u, cols], row_words[:, cols], ident[:])
+
+        def group_z(h):
+            nc.scalar.copy(z_words[:, :, h * 64 : (h + 1) * 64, :], back[h][:].rearrange("p u (m t) -> p t m u", t=PACK))
 
         make_yd(0)
         make_yd(1)
         look_up(0)
-        clip(0)
         make_yd(2)
-        add_up(0)
+        add_plain(0)
+        add_plain(1)
+        clip(0)
         look_up(1)
-        clip(1)
         make_yd(3)
-        add_up(1)
         make_b(3)
-        turn_back(0)
+        make_gate(3)
+        add_clipped(0)
+        add_plain(2)
+        clip(1)
+        add_clipped(1)
+        add_plain(3)
+        scale_b(0)
+        scale_b(1)
         look_up(2)
+        last_bf = clipped[3][:].bitcast(BF16)
+        for h in range(2):
+            turn_back(0, h, last_bf[:, (2 + h) * N : (3 + h) * N])
         clip(2)
-        add_up(2)
-        for t in range(PACK - 1):
-            scale_b(t)
+        add_clipped(2)
+        scale_b(2)
         look_up(3)
         pa_last = d_win[3][:, N : N + HALF]
         fetch_pa(3, pa_last)
         clip(3)
-        add_up(3)
+        add_clipped(3)
         put_back(3, pa_last)
-        turn_back(1)
-
-        z_grouped = sbuf("z_grouped", [P, PACK * N], BF16)
-        z_words = z_grouped[:].bitcast(F32).rearrange("p (t m u) -> p t m u", t=PACK, u=2)
         for h in range(2):
-            nc.scalar.copy(z_words[:, :, h * 64 : (h + 1) * 64, :], back[h][:].rearrange("p u (m t) -> p t m u", t=PACK))
+            turn_back(1, h, sbuf(f"zT_rows{h}", [P, N], BF16)[:])
+        for h in range(2):
+            group_z(h)
 
-        halves = [slice(0, HALF), slice(HALF, N)]
         for cols in halves:
             nc.vector.tensor_scalar(z2_planes[:, 3, cols], b_win[3][:, cols], gb_signed[:, 3:4], None, ALU.mult)
-        z2_grouped = sbuf("z2_grouped", [P, PACK * N], BF16)
-        dst = z2_grouped[:].rearrange("p (h c i t) -> p h c t i", h=2, i=4, t=PACK)
-        src = z2_planes[:].rearrange("p t (h c i) -> p h c t i", h=2, i=4)
-        for h in range(2):
-            nc.vector.tensor_copy(dst[:, h], src[:, h])
+        dst = z2_grouped[:].rearrange("p (c i t) -> p c t i", i=4, t=PACK)
+        src = z2_planes.rearrange("p t (c i) -> p c t i", i=4)
+        nc.vector.tensor_copy(dst[:, :64], src[:, :64])
+        nc.vector.tensor_copy(dst[:, 64:], src[:, 64:])
 
-        def quantize_pieces(name, grouped, edges):
-            codes = sbuf(f"{name}_codes", [P, N], U32)
-            scales = sbuf(f"{name}_scales", [P, N], U8)
-            for c0, c1 in zip(edges, edges[1:]):
-                nc.vector.quantize_mx(
-                    out=codes[:, c0:c1].bitcast(FP8X4), scales=scales[:, c0:c1], in_=grouped[:, PACK * c0 : PACK * c1]
-                )
-            return codes, scales
+        def quantize_columns(operand, grouped, c0, c1):
+            codes, scales = operand
+            nc.vector.quantize_mx(
+                out=codes[:, c0:c1].bitcast(FP8X4), scales=scales[:, c0:c1], in_=grouped[:, PACK * c0 : PACK * c1]
+            )
 
-        z2q = quantize_pieces("z2", z2_grouped, [0, HALF, N])
-        zq = quantize_pieces("z", z_grouped, [0, P, 2 * P, N])
+        z2q = (sbuf("z2_codes", [P, N], U32), sbuf("z2_scales", [P, N], U8))
+        zq = (sbuf("z_codes", [P, N], U32), sbuf("z_scales", [P, N], U8))
+        quantize_columns(z2q, z2_grouped, 0, HALF)
+        quantize_columns(zq, z_grouped, 0, P)
+        quantize_columns(z2q, z2_grouped, HALF, N)
+        quantize_columns(zq, z_grouped, P, 2 * P)
+        quantize_columns(zq, z_grouped, 2 * P, N)
 
         out_rows = out.rearrange("(p t) v -> t p v", t=PACK)
         for t in range(PACK):
             rows = slice(t * P, (t + 1) * P)
             for i, cols in enumerate(halves if t == 0 else [slice(0, N)]):
                 width = cols.stop - cols.start
-                if t == 0:
-                    acc = bank(f"s0{i}", [P, width])
-                else:
-                    acc = psum.tile([P, width], F32, name=f"s{t}", tag=f"zT{t}")
+                acc = bank(f"s{t}{i}", [P, width])
                 nc.tensor.matmul_mx(
                     out=acc[:], lhsT=zq[0][:, rows].bitcast(FP8X4), lhsT_scale=zq[1][:, rows],
                     rhs=z2q[0][:, cols].bitcast(FP8X4), rhs_scale=z2q[1][:, cols], start=True, stop=True,
                 )
                 nc.scalar.activation(y_win[t][:, cols], acc[:], ACT.Copy, scale=0.0625)
-        sg = dgs + ygs
+        sg = [gap_tiles[t // 2][:, (t % 2) * N : (t % 2 + 1) * N] for t in range(PACK)]
         for t in range(PACK + 1):
             if t < PACK:
-                nc.vector.tensor_copy(sg[t][:], y_win[t][:].indirect(n5_t[:]))
+                nc.vector.tensor_copy(sg[t], y_win[t][:].indirect(n5_t[:]))
             if t > 0:
                 for cols in halves if t == PACK else [slice(0, N)]:
                     res = d_win[t - 1][:, cols]

from contextlib import ExitStack

import concourse.mybir as mybir
from concourse.masks import make_identity

F32 = mybir.dt.float32
BF16 = mybir.dt.bfloat16
I32 = mybir.dt.int32
U32 = mybir.dt.uint32
U16 = mybir.dt.uint16
U8 = mybir.dt.uint8
FP8X4 = mybir.dt.float8_e4m3fn_x4
ALU = mybir.AluOpType
ACT = mybir.ActivationFunctionType

P = 128
PACK = 4
T = 2048
N = 512
HALF = N // 2
WIDE = 2 * N

FLOPS = 4 * 2 * 512 * 512 * 512


def tile_picked_twkmaxbfoldbig_none_p_kernel(
    tc, x_words, x_scales, w1, w2, w3, ga, gb, offs, two, n1, n2, three, n3, n4, n5, out
):
    nc = tc.nc
    with ExitStack() as ctx:
        keep = ctx.enter_context(tc.tile_pool(name="keep", bufs=1))
        psum = ctx.enter_context(tc.psum_pool(name="psum", bufs=1))

        def sbuf(name, shape, dtype):
            return keep.tile(shape, dtype, name=name, align_bytes=64)

        def bank(name, shape):
            return psum.tile(shape, F32, name=name, tag="ring", bufs=4)

        def load_list(name, src):
            tile = sbuf(name, list(src.shape), U16)
            nc.sync.dma_start(tile[:], src)
            return tile

        def load_weight(name, w, pieces):
            rows = w.rearrange("(p j) c -> p j c", j=PACK)
            width = N // pieces
            halves = []
            for i in range(pieces):
                raw = sbuf(f"{name}_raw{i}", [P, PACK, width], F32)
                nc.sync.dma_start(raw[:], rows[:, :, i * width : (i + 1) * width])
                halves.extend(raw[:, :, c : c + HALF] for c in range(0, width, HALF))
            return halves

        scale_rows = sbuf("scale_rows", [P, T], U8)
        nc.vector.memset(scale_rows[:, : T // 2].bitcast(I32), 0)
        nc.gpsimd.memset(scale_rows[:, T // 2 :].bitcast(I32), 0)
        warm = sbuf("warm", [P, 2], F32)
        nc.gpsimd.memset(warm[:, 0:1], 0.0)
        nc.scalar.activation(warm[:, 1:2], warm[:, 0:1], ACT.Sigmoid)

        three_t = load_list("three_t", three)
        offs_t = load_list("offs_t", offs)
        two_t = load_list("two_t", two)
        for q in range(4):
            nc.sync.dma_start(scale_rows[32 * q : 32 * q + 4, :].bitcast(I32), x_scales[0, 4 * q : 4 * q + 4, :].bitcast(I32))
        words = sbuf("words", [P, T], U32)
        w3_raw = load_weight("w3", w3, 2)
        nc.sync.dma_start(words[:].bitcast(I32), x_words[0].rearrange("p c r -> p (c r)").bitcast(I32))
        n4_t = load_list("n4_t", n4)
        n3_t = load_list("n3_t", n3)
        w1_raw = load_weight("w1", w1, 2)
        w2_raw = load_weight("w2", w2, 2)
        n2_t = load_list("n2_t", n2)
        n1_t = load_list("n1_t", n1)
        n5_t = load_list("n5_t", n5)

        ga_t = sbuf("ga_t", [P, PACK], F32)
        gb_t = sbuf("gb_t", [P, PACK], F32)
        nc.gpsimd.dma_start(ga_t[:], ga.rearrange("(p t) o -> p (t o)", t=PACK))
        nc.gpsimd.dma_start(gb_t[:], gb.rearrange("(p t) o -> p (t o)", t=PACK))
        sign2 = sbuf("sign2", [P, PACK], F32)
        sign = sbuf("sign", [P, PACK], F32)
        ga_abs = sbuf("ga_abs", [P, PACK], F32)
        ga_neg = sbuf("ga_neg", [P, PACK], F32)
        gb_signed = sbuf("gb_signed", [P, PACK], F32)
        nc.gpsimd.tensor_scalar(sign2[:], ga_t[:], 0.0, 2.0, ALU.is_ge, ALU.mult)
        nc.gpsimd.tensor_scalar(sign[:], sign2[:], 1.0, -1.0, ALU.mult, ALU.add)
        nc.gpsimd.tensor_tensor(ga_abs[:], ga_t[:], sign[:], ALU.mult)
        nc.gpsimd.tensor_scalar(ga_neg[:], ga_abs[:], -1.0, 0.0, ALU.mult, ALU.add)
        nc.gpsimd.tensor_tensor(gb_signed[:], gb_t[:], sign[:], ALU.mult)
        ident = sbuf("ident", [P, P], F32)
        make_identity(nc, ident[:])

        y_win = [sbuf(f"y_win{t}", [P, WIDE], F32) for t in range(PACK)]
        d_win = [sbuf(f"d_win{t}", [P, WIDE], F32) for t in range(PACK)]

        def pick_bytes(name, lst):
            tile = sbuf(name, [P, N], U8)
            nc.vector.tensor_copy(tile[:], scale_rows[:].indirect(lst[:]))
            return tile

        def pick_words(name, lst):
            tile = sbuf(name, [P, N], U32)
            nc.vector.tensor_copy(tile[:], words[:].indirect(lst[:]))
            return tile

        def quantize(name, grouped):
            codes = sbuf(f"{name}_codes", [P, N], U32)
            scales = sbuf(f"{name}_scales", [P, N], U8)
            nc.vector.quantize_mx(out=codes[:].bitcast(FP8X4), scales=scales[:], in_=grouped[:])
            return codes, scales

        def group_weight(name, raw):
            grouped = sbuf(f"{name}_grouped", [P, PACK * N], BF16)
            view = grouped[:].rearrange("p (t m j) -> p m j t", t=PACK, j=PACK)
            for h in range(2):
                nc.scalar.copy(view[:, h * 64 : (h + 1) * 64], raw[h].rearrange("p j (m t) -> p m j t", t=PACK))
            return grouped

        def product(name, stat, mov, t):
            acc = bank(name, [P, N])
            cols = slice(t * P, (t + 1) * P)
            nc.tensor.matmul_mx(
                out=acc[:], lhsT=stat[0][:, cols].bitcast(FP8X4), lhsT_scale=stat[1][:, cols],
                rhs=mov[0][:].bitcast(FP8X4), rhs_scale=mov[1][:], start=True, stop=True,
            )
            return acc

        xb_bytes = pick_bytes("xb_bytes", three_t)
        xy_bytes = pick_bytes("xy_bytes", offs_t)
        xd_bytes = pick_bytes("xd_bytes", two_t)
        w3q = quantize("w3", group_weight("w3", w3_raw))
        xb = (pick_words("xb_words", three_t), xb_bytes)
        xy = (pick_words("xy_words", offs_t), xy_bytes)
        xd = (pick_words("xd_words", two_t), xd_bytes)

        gap_tiles = [sbuf(f"gaps{i}", [P, WIDE], F32) for i in range(2)]
        z2_planes = w2_raw[1].bitcast(BF16)
        b_win = [sbuf(f"b_win{t}", [P, N], F32) for t in range(PACK)]
        gate = [w2_raw[1][:, 3, :] if t == 2 else sbuf(f"gate{t}", [P, HALF], F32)[:] for t in range(PACK)]

        def make_b(t):
            acc = product(f"b{t}", w3q, xb, t)
            nc.scalar.copy(b_win[t][:], acc[:])

        def make_gate(t):
            nc.scalar.activation(gate[t], b_win[t][:].indirect(n4_t[:]), ACT.Sigmoid)

        def fetch_pa(t, pa):
            nc.vector.tensor_copy(pa, b_win[t][:].indirect(n3_t[:]))

        def put_back(t, pa):
            nc.vector.tensor_tensor(b_win[t][:].indirect(n4_t[:]), pa, gate[t], ALU.mult)

        def scale_b(t):
            nc.scalar.activation(z2_planes[:, t, :], b_win[t][:], ACT.Copy, scale=gb_signed[:, t : t + 1])

        pa_tiles = [sbuf(f"pa{t}", [P, HALF], F32) for t in range(2)]
        for step in (make_b, make_gate):
            for t in range(2):
                step(t)
        for step in (fetch_pa, put_back):
            for t in range(2):
                step(t, pa_tiles[t][:])

        w1_grouped = group_weight("w1", w1_raw)
        make_b(2)
        w1q = quantize("w1", w1_grouped)
        pa_third = w1_grouped[:].bitcast(F32)[:, :HALF]
        fetch_pa(2, pa_third)
        w2q = quantize("w2", group_weight("w2", w2_raw))
        make_gate(2)
        put_back(2, pa_third)

        zT = [[psum.tile([P, 2, 2, P], F32, name=f"zT{u}{h}", tag=f"zT{u}{h}") for h in range(2)] for u in range(2)]
        back = [None, None]
        halves = [slice(0, HALF), slice(HALF, N)]
        clipped = [sbuf(f"clipped{t}", [P, WIDE], F32) for t in range(PACK)]

        def make_yd(t):
            acc_d = product(f"d{t}", w2q, xd, t)
            nc.scalar.activation(d_win[t][:, :N], acc_d[:], ACT.Copy, scale=ga_neg[:, t : t + 1])
            acc_y = product(f"y{t}", w1q, xy, t)
            nc.scalar.activation(y_win[t][:, :N], acc_y[:], ACT.Copy, scale=ga_abs[:, t : t + 1])

        def look_up(t):
            gaps = gap_tiles[t % 2]
            nc.vector.tensor_tensor(gaps[:, :N], y_win[t][:].indirect(n1_t[:]), d_win[t][:, :N], ALU.add)
            nc.vector.tensor_tensor(gaps[:, N:], d_win[t][:].indirect(n2_t[:]), y_win[t][:, :N], ALU.add)

        def clip(t):
            gaps = gap_tiles[t % 2]
            if t < 2:
                nc.scalar.activation(clipped[t][:], gaps[:], ACT.Relu, scale=-1.0)
            else:
                nc.vector.tensor_scalar(clipped[t][:, :N], gaps[:, :N], -1.0, 0.0, ALU.mult, ALU.max)
                nc.scalar.activation(clipped[t][:, N:], gaps[:, N:], ACT.Relu, scale=-1.0)

        def add_term(t, h, term, first=False, last=False):
            for cc in range(2):
                nc.tensor.matmul(
                    zT[t // 2][h][:, cc, t % 2, :], term[:, cc * P : (cc + 1) * P], ident[:], is_transpose=True,
                    start=(first and t % 2 == 0 and cc == 0), stop=(last and t % 2 == 1 and cc == 1),
                )

        def add_plain(t):
            for h, cols in enumerate(halves):
                add_term(t, h, d_win[t][:, cols], first=True)
                add_term(t, h, y_win[t][:, cols])

        def add_clipped(t):
            for h, cols in enumerate(halves):
                add_term(t, h, clipped[t][:, :N][:, cols])
            for h, cols in enumerate(halves):
                add_term(t, h, clipped[t][:, N:][:, cols], last=True)

        z2_grouped = sbuf("z2_grouped", [P, PACK * N], BF16)
        z_grouped = sbuf("z_grouped", [P, PACK * N], BF16)
        z_words = z_grouped[:].bitcast(F32).rearrange("p (t m u) -> p t m u", t=PACK, u=2)

        def turn_back(u, h, rows):
            nc.scalar.copy(
                rows.rearrange("k (c p e) -> k c p e", c=2, e=2),
                zT[u][h][:].rearrange("k c e p -> k c p e"),
            )
            if u == 0:
                back[h] = psum.tile([P, 2, HALF], F32, name=f"back{h}", tag=f"zT0{h}")
            row_words = rows.bitcast(F32)
            for cc in range(2):
                cols = slice(cc * P, (cc + 1) * P)
                nc.tensor.transpose(back[h][:, u, cols], row_words[:, cols], ident[:])

        def group_z(h):
            nc.scalar.copy(z_words[:, :, h * 64 : (h + 1) * 64, :], back[h][:].rearrange("p u (m t) -> p t m u", t=PACK))

        make_yd(0)
        make_yd(1)
        look_up(0)
        make_yd(2)
        add_plain(0)
        add_plain(1)
        clip(0)
        look_up(1)
        make_yd(3)
        make_b(3)
        make_gate(3)
        add_clipped(0)
        add_plain(2)
        clip(1)
        add_clipped(1)
        add_plain(3)
        scale_b(0)
        scale_b(1)
        look_up(2)
        last_bf = clipped[3][:].bitcast(BF16)
        for h in range(2):
            turn_back(0, h, last_bf[:, (2 + h) * N : (3 + h) * N])
        clip(2)
        add_clipped(2)
        scale_b(2)
        look_up(3)
        pa_last = d_win[3][:, N : N + HALF]
        fetch_pa(3, pa_last)
        clip(3)
        add_clipped(3)
        put_back(3, pa_last)
        for h in range(2):
            turn_back(1, h, sbuf(f"zT_rows{h}", [P, N], BF16)[:])
        for h in range(2):
            group_z(h)

        for cols in halves:
            nc.vector.tensor_scalar(z2_planes[:, 3, cols], b_win[3][:, cols], gb_signed[:, 3:4], None, ALU.mult)
        dst = z2_grouped[:].rearrange("p (c i t) -> p c t i", i=4, t=PACK)
        src = z2_planes.rearrange("p t (c i) -> p c t i", i=4)
        nc.vector.tensor_copy(dst[:, :64], src[:, :64])
        nc.vector.tensor_copy(dst[:, 64:], src[:, 64:])

        def quantize_columns(operand, grouped, c0, c1):
            codes, scales = operand
            nc.vector.quantize_mx(
                out=codes[:, c0:c1].bitcast(FP8X4), scales=scales[:, c0:c1], in_=grouped[:, PACK * c0 : PACK * c1]
            )

        z2q = (sbuf("z2_codes", [P, N], U32), sbuf("z2_scales", [P, N], U8))
        zq = (sbuf("z_codes", [P, N], U32), sbuf("z_scales", [P, N], U8))
        quantize_columns(z2q, z2_grouped, 0, HALF)
        quantize_columns(zq, z_grouped, 0, P)
        quantize_columns(z2q, z2_grouped, HALF, N)
        quantize_columns(zq, z_grouped, P, 2 * P)
        quantize_columns(zq, z_grouped, 2 * P, N)

        out_rows = out.rearrange("(p t) v -> t p v", t=PACK)
        for t in range(PACK):
            rows = slice(t * P, (t + 1) * P)
            for i, cols in enumerate(halves if t == 0 else [slice(0, N)]):
                width = cols.stop - cols.start
                acc = bank(f"s{t}{i}", [P, width])
                nc.tensor.matmul_mx(
                    out=acc[:], lhsT=zq[0][:, rows].bitcast(FP8X4), lhsT_scale=zq[1][:, rows],
                    rhs=z2q[0][:, cols].bitcast(FP8X4), rhs_scale=z2q[1][:, cols], start=True, stop=True,
                )
                nc.scalar.activation(y_win[t][:, cols], acc[:], ACT.Copy, scale=0.0625)
        sg = [gap_tiles[t // 2][:, (t % 2) * N : (t % 2 + 1) * N] for t in range(PACK)]
        for t in range(PACK + 1):
            if t < PACK:
                nc.vector.tensor_copy(sg[t], y_win[t][:].indirect(n5_t[:]))
            if t > 0:
                for cols in halves if t == PACK else [slice(0, N)]:
                    res = d_win[t - 1][:, cols]
                    nc.vector.tensor_tensor(res, sg[t - 1][:, cols], y_win[t - 1][:, cols], ALU.max)
                    nc.sync.dma_start(out_rows[t - 1][:, cols], res)
